import numpy as np, ml_dtypes
CORES = [2,10,50,58,66,74,122]
N = 7
TOK, K = 512, 2
ROUTE = [[[1,4],[3,5],[1,5],[3,6],[3,4],[1,5],[0,6],[1,4],[5,6],[2,4],[0,5],[4,6],[3,6],[1,2],[2,4],[1,5],[3,4],[2,5],[2,3],[2,6],[2,4],[0,1],[3,6],[2,5],[2,5],[3,5],[2,3],[0,3],[1,4],[2,6],[3,5],[0,4],[3,4],[1,3],[4,6],[2,6],[5,6],[0,1],[5,6],[1,6],[1,5],[0,6],[0,3],[4,5],[0,3],[1,4],[4,6],[0,1],[2,5],[5,6],[0,4],[2,3],[0,6],[0,1],[0,2],[0,1],[0,2],[0,4],[4,5],[2,5],[0,1],[0,1],[4,5],[3,4],[0,4],[2,3],[0,6],[0,5],[1,5],[5,6],[5,6],[0,1],[2,5],[3,5],[3,5],[0,2],[2,6],[4,6],[0,5],[2,6],[1,3],[1,5],[3,4],[3,5],[0,4],[3,6],[1,3],[2,6],[0,3],[5,6],[0,6],[4,5],[0,1],[3,4],[0,4],[1,5],[2,5],[1,5],[4,5],[1,4],[4,6],[0,6],[1,2],[5,6],[1,2],[1,2],[0,4],[3,5],[0,1],[2,5],[3,6],[3,4],[4,5],[0,5],[0,4],[1,5],[2,5],[1,5],[0,3],[1,4],[4,6],[1,3],[3,5],[1,2],[2,3],[1,5],[2,3],[1,6],[1,4],[1,5],[1,3],[0,3],[1,6],[3,5],[3,6],[1,4],[1,6],[2,6],[3,6],[1,4],[0,1],[3,5],[3,5],[0,6],[1,4],[2,5],[0,4],[2,6],[5,6],[0,6],[1,6],[0,1],[0,6],[1,5],[1,3],[2,5],[2,5],[1,2],[1,6],[0,1],[1,5],[3,6],[1,4],[1,2],[1,2],[0,2],[2,6],[0,1],[1,6],[2,4],[1,3],[3,5],[1,3],[0,4],[3,6],[0,2],[0,2],[1,6],[4,5],[0,5],[2,5],[0,1],[0,2],[3,4],[1,4],[3,6],[2,4],[1,4],[2,5],[4,5],[1,6],[3,4],[0,5],[4,6],[0,4],[1,3],[1,3],[2,4],[0,2],[1,6],[0,3],[0,6],[3,4],[0,3],[4,5],[1,3],[2,4],[1,3],[4,6],[1,5],[4,6],[0,6],[4,6],[1,2],[1,3],[1,4],[1,5],[5,6],[2,3],[0,4],[0,1],[3,4],[0,3],[4,5],[4,5],[4,5],[1,2],[0,3],[0,3],[1,5],[1,5],[4,5],[2,6],[0,5],[0,4],[2,5],[2,6],[2,3],[0,1],[0,3],[1,6],[2,5],[4,5],[3,4],[2,5],[4,6],[1,4],[2,5],[0,5],[1,2],[4,6],[2,3],[0,4],[0,2],[0,2],[3,6],[1,3],[2,3],[3,4],[0,6],[0,4],[0,2],[0,5],[0,4],[0,5],[4,5],[3,4],[0,5],[1,3],[0,2],[3,4],[2,6],[1,4],[2,4],[0,2],[0,4],[3,6],[1,4],[3,5],[1,5],[2,6],[0,1],[3,5],[0,3],[5,6],[4,6],[0,4],[2,4],[2,3],[0,3],[4,6],[1,6],[0,5],[5,6],[1,2],[0,5],[5,6],[3,5],[0,2],[3,6],[3,6],[2,5],[5,6],[0,6],[2,6],[0,5],[1,2],[1,6],[0,1],[1,6],[0,3],[1,3],[2,3],[1,4],[4,5],[3,4],[3,4],[2,6],[0,4],[4,6],[0,5],[5,6],[3,4],[0,1],[1,4],[1,5],[1,6],[0,2],[1,3],[0,3],[0,1],[2,3],[3,4],[2,4],[2,3],[1,3],[0,4],[0,2],[2,6],[0,2],[3,6],[3,5],[5,6],[0,2],[0,6],[2,3],[0,6],[5,6],[4,5],[4,6],[4,6],[2,5],[1,5],[4,5],[2,5],[2,5],[1,2],[1,5],[4,5],[1,2],[0,3],[5,6],[2,5],[3,5],[4,6],[4,6],[4,6],[0,4],[0,4],[2,6],[1,6],[2,3],[2,6],[3,5],[3,6],[4,5],[0,1],[1,5],[3,5],[4,6],[4,5],[1,6],[3,6],[0,4],[2,3],[2,4],[0,1],[5,6],[0,6],[4,5],[0,5],[0,1],[2,4],[2,5],[0,6],[2,5],[0,3],[2,5],[4,5],[1,6],[0,5],[3,5],[1,2],[2,3],[2,3],[3,4],[4,6],[0,1],[0,4],[0,1],[3,5],[3,6],[5,6],[2,5],[3,4],[3,6],[0,3],[2,6],[0,3],[4,5],[2,4],[1,5],[2,4],[2,5],[0,4],[1,4],[1,4],[3,6],[2,3],[3,5],[1,5],[4,6],[2,3],[0,4],[5,6],[4,6],[1,3],[0,5],[1,3],[2,4],[1,4],[2,4],[2,4],[0,3],[2,5],[0,4],[5,6],[4,5],[3,6],[2,6],[2,5],[2,4],[1,3],[3,6],[0,6],[1,4],[4,5],[4,6],[0,2],[0,5],[0,6],[2,3],[5,6],[1,5],[3,6],[4,5],[2,5],[1,6],[1,4],[0,6],[2,4],[1,4],[4,6],[0,2],[1,3],[4,6],[0,2],[3,6],[3,5],[3,6],[1,2],[2,5],[0,3],[0,3],[2,3],[0,3],[4,5],[4,5],[3,6],[0,2],[0,5],[2,3],[0,6],[0,3],[2,5],[0,4],[2,3],[3,4],[3,5],[0,3],[0,2],[1,4],[3,4],[1,5],[0,2],[0,5],[3,6],[3,6],[3,5],[3,6],[0,3],[1,3]],[[1,3],[3,6],[3,4],[2,6],[2,4],[3,5],[0,2],[1,4],[3,6],[1,4],[4,6],[2,3],[0,4],[3,4],[3,4],[3,4],[2,4],[0,5],[4,6],[0,1],[2,4],[1,2],[1,6],[1,6],[3,6],[2,6],[4,6],[2,6],[2,6],[0,1],[2,5],[5,6],[2,5],[2,3],[0,1],[1,5],[1,4],[4,6],[2,4],[2,5],[2,4],[1,6],[5,6],[5,6],[1,6],[3,6],[2,4],[1,2],[4,5],[1,5],[0,3],[1,5],[4,5],[2,6],[0,1],[2,6],[3,6],[1,2],[3,5],[0,1],[3,6],[1,6],[0,2],[4,6],[3,4],[2,6],[3,4],[0,4],[0,5],[0,6],[0,5],[4,5],[5,6],[3,6],[3,4],[1,4],[2,4],[2,4],[0,5],[1,2],[2,3],[3,5],[3,6],[2,4],[1,3],[2,4],[2,4],[2,3],[0,1],[2,4],[3,6],[0,5],[2,3],[0,1],[0,1],[1,2],[0,4],[2,5],[0,1],[2,6],[3,5],[4,6],[3,4],[1,4],[0,5],[0,1],[0,5],[1,4],[2,4],[2,5],[2,3],[4,5],[0,5],[5,6],[1,5],[1,3],[0,5],[3,4],[2,4],[0,2],[4,5],[2,5],[3,5],[0,5],[0,1],[0,5],[0,6],[0,2],[1,6],[1,4],[2,3],[2,3],[4,5],[2,5],[0,4],[0,2],[0,2],[3,5],[0,1],[0,1],[2,5],[3,5],[1,4],[4,5],[0,6],[1,6],[2,4],[1,4],[3,6],[3,5],[1,2],[0,1],[2,5],[2,5],[2,6],[1,5],[2,5],[1,3],[2,5],[1,5],[0,1],[1,5],[3,6],[3,5],[0,1],[5,6],[0,4],[2,4],[5,6],[3,4],[2,5],[0,5],[0,6],[3,5],[0,6],[4,5],[2,5],[2,6],[2,6],[2,4],[3,4],[3,4],[0,2],[0,1],[0,1],[3,6],[4,6],[1,3],[1,4],[3,4],[1,4],[4,6],[2,5],[3,4],[0,6],[3,4],[2,5],[0,3],[2,4],[3,5],[1,5],[4,6],[0,2],[0,3],[1,4],[1,2],[0,4],[5,6],[4,6],[0,6],[3,5],[0,3],[1,4],[0,4],[0,6],[0,1],[1,6],[2,4],[0,2],[0,5],[0,5],[0,5],[0,6],[1,2],[4,5],[0,3],[0,5],[2,5],[2,3],[0,2],[2,4],[1,4],[3,5],[4,5],[3,4],[0,2],[2,6],[3,4],[1,5],[0,1],[3,4],[1,2],[0,4],[1,3],[4,5],[2,6],[0,1],[1,2],[1,6],[0,6],[2,4],[0,6],[1,6],[0,5],[1,6],[1,4],[3,6],[2,6],[0,1],[1,3],[0,5],[3,6],[3,4],[3,4],[2,5],[1,3],[4,6],[2,4],[1,3],[1,5],[1,5],[2,6],[3,4],[0,4],[2,5],[5,6],[2,3],[2,3],[1,2],[3,5],[1,3],[3,4],[0,1],[1,2],[1,6],[5,6],[2,5],[5,6],[2,3],[0,1],[5,6],[1,2],[1,4],[1,5],[2,4],[3,5],[0,5],[0,5],[3,4],[1,5],[2,3],[0,1],[0,1],[1,5],[1,3],[0,1],[3,6],[2,4],[5,6],[1,2],[4,6],[0,5],[1,6],[3,5],[1,3],[4,5],[2,5],[5,6],[2,5],[1,4],[0,5],[0,3],[2,4],[0,4],[3,5],[2,3],[1,5],[3,4],[4,5],[3,5],[4,6],[2,5],[3,5],[2,6],[0,2],[0,3],[4,6],[3,6],[0,4],[0,2],[0,4],[2,3],[1,6],[1,2],[1,3],[2,4],[1,6],[5,6],[0,4],[0,1],[1,4],[0,6],[4,5],[1,2],[1,2],[2,5],[1,5],[0,2],[0,1],[1,6],[3,5],[1,3],[0,6],[3,5],[0,1],[1,5],[0,5],[1,6],[2,3],[0,5],[3,4],[2,4],[2,3],[0,1],[0,1],[1,6],[0,6],[4,5],[4,5],[4,6],[5,6],[0,5],[4,6],[4,6],[1,6],[1,4],[1,2],[1,2],[3,6],[2,3],[3,6],[3,6],[0,3],[3,4],[4,6],[0,3],[0,6],[0,4],[2,6],[1,6],[3,5],[3,5],[0,4],[4,6],[1,4],[3,6],[3,5],[1,2],[1,4],[2,5],[1,6],[3,4],[5,6],[3,5],[0,6],[3,4],[2,6],[0,1],[2,5],[1,3],[2,3],[1,5],[3,4],[0,3],[1,2],[2,6],[4,5],[2,4],[1,5],[5,6],[0,1],[4,5],[2,3],[0,4],[4,6],[0,2],[1,3],[1,6],[0,6],[1,4],[1,2],[0,5],[1,5],[0,4],[4,6],[1,5],[0,2],[0,1],[0,5],[1,2],[0,6],[1,6],[2,6],[1,4],[0,3],[0,6],[1,5],[0,1],[0,6],[3,4],[2,4],[0,2],[1,3],[0,1],[0,5],[1,4],[4,6],[3,4],[2,6],[1,6],[2,3],[1,2],[0,6],[1,5],[0,5],[2,4],[0,2],[1,5],[2,6],[0,6],[1,2],[1,4],[2,5],[0,1],[4,5],[2,4],[1,4],[1,3],[2,5],[3,6],[5,6],[1,6],[4,5],[0,2],[3,6],[0,6],[5,6],[0,5],[1,3],[2,5],[1,6],[0,2],[0,5],[0,4],[0,4],[1,2],[1,2],[1,2],[2,6],[3,6],[0,3],[2,5]],[[0,5],[0,6],[5,6],[0,2],[2,3],[2,5],[4,6],[5,6],[1,3],[2,3],[3,4],[1,5],[0,4],[4,5],[0,6],[4,5],[4,6],[3,6],[0,4],[0,3],[2,3],[3,4],[1,4],[0,4],[1,4],[0,4],[2,3],[0,3],[2,5],[2,3],[1,3],[0,1],[2,3],[0,3],[2,3],[0,2],[3,4],[0,5],[1,5],[1,3],[3,5],[5,6],[1,5],[4,5],[0,3],[0,1],[0,6],[4,5],[0,2],[2,4],[5,6],[4,6],[4,6],[0,4],[2,4],[0,4],[1,3],[1,5],[0,6],[3,5],[2,4],[1,2],[0,2],[2,6],[2,5],[1,6],[0,1],[1,4],[3,5],[1,4],[2,5],[2,5],[2,6],[4,5],[0,3],[3,6],[3,4],[0,1],[0,2],[2,3],[1,3],[0,4],[1,6],[0,4],[5,6],[0,5],[2,6],[3,6],[0,4],[3,4],[4,5],[2,3],[3,4],[5,6],[0,6],[1,2],[2,6],[4,5],[0,1],[2,3],[1,5],[0,2],[2,3],[2,6],[1,6],[0,6],[1,2],[0,4],[2,3],[0,5],[1,2],[1,5],[4,5],[0,4],[2,4],[0,2],[1,2],[4,6],[1,2],[1,3],[3,6],[2,6],[0,3],[1,2],[2,3],[1,5],[3,4],[0,3],[1,4],[4,6],[2,6],[5,6],[2,4],[2,3],[4,5],[0,2],[2,5],[0,5],[2,5],[0,4],[0,2],[3,6],[0,2],[5,6],[2,5],[0,2],[0,2],[1,6],[0,1],[3,5],[0,4],[0,1],[2,5],[1,3],[2,3],[0,1],[0,3],[0,1],[1,2],[3,6],[0,2],[2,3],[4,6],[2,3],[4,5],[2,3],[3,4],[1,6],[3,4],[1,4],[1,6],[5,6],[1,5],[3,6],[0,2],[0,6],[1,2],[2,3],[2,5],[1,2],[1,5],[1,4],[1,5],[0,1],[1,5],[1,3],[1,5],[3,4],[2,6],[3,5],[1,6],[3,4],[2,5],[3,5],[2,4],[3,5],[0,5],[1,5],[0,3],[0,4],[1,2],[2,6],[4,5],[0,5],[1,2],[5,6],[0,2],[2,6],[4,5],[3,4],[1,3],[1,2],[0,4],[0,3],[1,3],[4,6],[5,6],[2,4],[0,3],[0,1],[4,5],[1,4],[1,6],[1,6],[0,2],[2,5],[0,4],[0,1],[3,4],[2,6],[4,5],[0,2],[4,6],[3,4],[0,1],[0,3],[1,5],[3,4],[3,6],[3,5],[2,5],[4,6],[0,6],[3,6],[2,6],[1,4],[2,5],[1,4],[1,2],[4,6],[0,3],[0,4],[0,6],[3,5],[2,5],[3,6],[3,6],[4,6],[0,1],[1,5],[3,4],[0,2],[4,5],[1,3],[2,5],[0,1],[3,5],[1,3],[1,4],[0,2],[1,2],[2,5],[0,6],[1,2],[3,4],[1,5],[0,2],[3,4],[1,2],[2,4],[0,6],[1,4],[1,2],[2,3],[2,5],[1,6],[1,6],[2,6],[0,2],[4,6],[5,6],[0,4],[1,3],[0,5],[2,3],[1,2],[0,6],[1,2],[4,6],[2,5],[1,3],[1,3],[1,3],[1,2],[0,1],[2,4],[0,6],[2,6],[0,1],[3,5],[1,2],[2,6],[2,5],[0,4],[0,3],[0,4],[5,6],[0,2],[1,4],[2,6],[3,4],[2,3],[1,5],[1,6],[1,2],[0,3],[4,6],[3,6],[4,5],[1,2],[4,5],[1,5],[2,3],[0,1],[1,6],[0,6],[0,3],[1,5],[1,2],[3,4],[5,6],[1,5],[2,5],[4,5],[4,5],[3,5],[4,6],[2,5],[0,4],[3,6],[1,6],[0,6],[1,6],[4,6],[1,3],[0,5],[0,4],[1,4],[3,6],[4,6],[1,4],[0,6],[0,6],[2,5],[1,3],[5,6],[5,6],[0,4],[0,5],[4,5],[1,3],[4,5],[0,4],[0,2],[3,5],[1,6],[0,4],[4,6],[0,4],[1,3],[0,2],[1,2],[2,4],[3,6],[3,4],[0,5],[0,2],[3,6],[2,3],[1,4],[0,5],[1,3],[0,4],[0,6],[1,2],[3,5],[0,3],[3,5],[0,5],[1,2],[1,6],[0,1],[0,4],[4,6],[4,5],[0,2],[3,4],[5,6],[0,5],[5,6],[1,2],[0,1],[0,3],[5,6],[1,6],[2,3],[1,2],[5,6],[1,4],[1,3],[3,6],[1,5],[1,6],[1,6],[0,2],[0,6],[1,2],[2,5],[3,6],[1,5],[2,3],[0,4],[0,3],[3,4],[2,5],[0,3],[1,6],[2,5],[1,5],[4,6],[2,6],[2,5],[4,6],[3,4],[0,4],[1,6],[3,5],[1,4],[1,5],[2,6],[3,5],[0,2],[0,4],[1,2],[4,5],[0,4],[2,3],[1,4],[2,3],[4,6],[1,3],[2,5],[2,3],[1,5],[0,3],[0,2],[2,6],[4,5],[2,5],[4,5],[2,4],[1,2],[3,6],[2,3],[0,3],[5,6],[0,2],[3,6],[1,2],[0,1],[3,4],[0,5],[5,6],[0,3],[0,5],[0,5],[0,4],[4,6],[2,6],[1,6],[3,5],[5,6],[2,4],[0,4],[4,6],[0,5],[0,5],[0,3],[3,6],[0,3],[4,6],[1,4],[0,1],[1,2],[0,3],[2,6],[5,6],[3,4],[1,6],[0,3],[0,5],[2,3]],[[0,2],[1,6],[1,4],[0,6],[2,3],[1,6],[1,6],[1,4],[3,4],[3,6],[0,4],[4,6],[1,6],[0,2],[1,5],[0,3],[0,4],[2,5],[0,5],[1,6],[0,3],[0,2],[4,6],[2,4],[3,5],[0,6],[2,4],[1,4],[2,5],[0,3],[4,5],[3,5],[4,5],[4,6],[1,4],[1,3],[1,3],[2,6],[3,6],[2,6],[1,2],[0,2],[2,4],[4,6],[0,6],[3,6],[3,4],[0,5],[0,6],[2,6],[2,5],[1,3],[1,5],[1,4],[2,4],[0,4],[1,3],[1,2],[1,5],[0,3],[2,4],[4,5],[5,6],[0,3],[0,3],[3,6],[5,6],[4,5],[0,1],[0,4],[2,4],[5,6],[1,3],[3,4],[1,6],[2,3],[0,2],[0,4],[0,1],[5,6],[2,5],[2,3],[0,2],[1,4],[2,3],[1,4],[0,2],[0,1],[2,3],[5,6],[0,4],[3,4],[3,6],[0,1],[1,2],[4,6],[4,5],[2,6],[2,5],[2,5],[1,6],[2,5],[3,6],[3,5],[0,6],[1,6],[4,5],[1,2],[5,6],[1,4],[3,6],[2,6],[1,6],[3,5],[2,3],[4,6],[4,5],[0,1],[1,3],[4,6],[2,5],[3,4],[1,5],[3,4],[1,3],[1,3],[2,4],[3,5],[1,5],[4,6],[1,5],[0,1],[5,6],[1,2],[0,5],[0,3],[0,1],[2,4],[0,3],[3,6],[2,5],[4,5],[0,4],[2,6],[0,1],[2,5],[1,4],[0,2],[2,5],[2,3],[0,6],[1,3],[1,6],[0,6],[3,5],[5,6],[2,6],[4,5],[3,6],[0,6],[4,5],[3,4],[2,5],[0,3],[0,5],[0,1],[2,4],[0,6],[0,4],[2,3],[1,6],[3,6],[0,4],[1,4],[2,3],[5,6],[1,6],[0,4],[2,3],[0,3],[2,3],[3,6],[2,5],[1,5],[0,4],[4,5],[2,3],[1,3],[1,3],[2,5],[1,5],[0,4],[0,3],[2,3],[0,4],[0,2],[1,3],[2,5],[0,4],[1,4],[4,5],[4,5],[1,6],[0,5],[2,5],[1,5],[2,6],[1,4],[0,1],[3,6],[0,5],[1,4],[4,6],[5,6],[0,2],[2,4],[0,5],[0,2],[2,5],[1,5],[1,5],[0,4],[2,5],[0,3],[1,2],[5,6],[1,4],[0,3],[2,6],[1,4],[0,2],[0,5],[1,5],[0,6],[0,6],[3,4],[0,6],[0,1],[0,3],[0,4],[1,6],[1,4],[0,3],[0,2],[4,5],[1,2],[1,3],[0,3],[0,1],[1,2],[1,3],[0,5],[4,5],[2,3],[0,4],[1,3],[1,4],[1,4],[0,1],[1,2],[5,6],[0,6],[4,5],[2,6],[0,2],[2,3],[1,6],[0,4],[4,5],[0,2],[3,5],[5,6],[0,1],[1,2],[4,6],[1,5],[0,4],[2,4],[0,1],[4,6],[0,5],[1,3],[1,4],[3,6],[5,6],[0,1],[1,6],[1,6],[2,3],[4,5],[0,3],[0,4],[4,6],[4,6],[5,6],[0,6],[0,2],[4,6],[3,4],[2,3],[1,3],[1,6],[3,5],[0,4],[0,2],[1,5],[0,3],[1,4],[2,3],[1,3],[0,2],[3,5],[0,5],[3,5],[4,6],[1,6],[1,6],[3,4],[2,3],[2,4],[3,4],[1,4],[1,5],[0,1],[0,3],[4,5],[0,6],[4,5],[4,6],[2,5],[1,2],[0,2],[3,6],[4,6],[1,3],[0,4],[1,4],[0,4],[2,6],[1,6],[0,1],[3,6],[2,5],[0,4],[2,4],[3,5],[0,2],[0,3],[1,2],[1,3],[0,5],[2,3],[0,4],[2,6],[0,5],[0,1],[2,4],[2,6],[0,2],[1,4],[0,6],[0,4],[0,3],[3,4],[0,6],[2,6],[3,5],[3,4],[0,4],[0,4],[2,3],[2,3],[0,3],[3,6],[0,3],[0,5],[1,6],[0,4],[1,5],[3,6],[1,5],[4,5],[1,4],[1,3],[3,6],[1,2],[2,5],[1,2],[2,6],[0,3],[2,5],[4,6],[2,3],[3,6],[2,4],[4,5],[1,2],[0,4],[3,4],[4,5],[1,6],[1,4],[1,2],[3,5],[0,6],[2,6],[0,2],[2,6],[0,4],[2,3],[2,4],[3,5],[3,5],[1,4],[1,4],[3,6],[1,2],[0,6],[2,3],[2,6],[3,5],[3,6],[1,3],[0,3],[0,5],[0,4],[3,4],[0,6],[0,2],[0,2],[2,3],[1,6],[0,3],[0,2],[0,1],[2,5],[0,6],[0,3],[2,4],[3,4],[1,4],[0,2],[0,4],[2,4],[5,6],[1,2],[1,6],[1,6],[2,5],[0,1],[0,4],[5,6],[2,6],[3,5],[2,3],[4,6],[1,3],[5,6],[2,6],[1,4],[2,3],[2,5],[4,5],[0,2],[0,1],[4,5],[1,6],[1,2],[2,5],[1,5],[1,6],[1,2],[4,6],[4,5],[1,5],[1,2],[4,5],[1,6],[3,6],[0,1],[3,4],[4,6],[2,5],[4,5],[1,6],[2,4],[5,6],[0,3],[1,2],[0,2],[1,5],[0,1],[0,1],[1,5],[3,6],[2,6],[0,3],[1,5],[4,5],[1,4],[1,6],[4,6],[2,4],[0,6],[1,6],[5,6],[1,3],[2,3],[3,6],[1,5],[0,4],[2,4]],[[2,5],[1,6],[1,2],[1,6],[1,3],[4,6],[0,3],[0,2],[4,5],[0,6],[2,6],[4,6],[0,1],[1,2],[0,3],[0,2],[0,1],[2,5],[3,4],[0,6],[0,4],[2,6],[0,4],[0,4],[4,5],[0,4],[2,4],[0,6],[1,4],[2,4],[0,2],[2,4],[1,6],[0,6],[0,4],[3,4],[1,6],[1,4],[2,5],[4,6],[2,6],[2,4],[1,4],[3,5],[0,5],[2,3],[0,3],[5,6],[0,3],[2,6],[3,5],[3,5],[0,2],[2,3],[1,2],[0,1],[4,5],[2,6],[3,6],[1,4],[1,3],[1,2],[1,5],[4,6],[3,6],[1,3],[1,4],[3,4],[1,4],[1,5],[2,3],[1,6],[4,6],[1,3],[2,6],[1,4],[2,5],[2,5],[0,3],[0,3],[2,5],[2,5],[4,5],[4,5],[2,4],[3,4],[0,1],[1,4],[0,6],[1,4],[1,3],[3,4],[2,4],[5,6],[2,3],[2,3],[1,6],[0,6],[0,6],[4,5],[1,4],[0,3],[0,1],[0,6],[0,4],[0,2],[3,6],[1,3],[2,6],[1,2],[4,6],[0,2],[2,5],[0,2],[0,4],[1,2],[3,6],[4,6],[1,4],[3,4],[0,1],[4,6],[4,6],[0,4],[0,3],[2,5],[4,6],[3,4],[4,5],[1,6],[2,5],[4,5],[4,6],[0,3],[3,5],[1,6],[0,4],[1,4],[0,4],[0,2],[1,5],[1,5],[0,3],[1,4],[3,4],[1,6],[3,5],[3,4],[1,3],[5,6],[0,1],[5,6],[2,4],[2,5],[0,2],[3,4],[3,4],[1,4],[0,3],[1,2],[2,3],[0,4],[2,3],[3,5],[2,6],[2,6],[0,5],[0,3],[3,6],[5,6],[3,4],[4,6],[1,4],[1,5],[0,4],[1,6],[5,6],[5,6],[0,4],[1,4],[0,6],[1,6],[3,6],[0,4],[2,3],[4,6],[3,5],[1,4],[1,4],[1,5],[5,6],[2,4],[1,4],[0,5],[2,6],[1,3],[0,2],[0,6],[0,5],[2,5],[1,3],[1,6],[1,2],[2,6],[0,2],[0,3],[3,5],[2,5],[2,6],[5,6],[3,6],[2,4],[3,6],[1,5],[1,6],[5,6],[3,4],[0,1],[2,3],[4,5],[3,5],[1,4],[2,3],[0,3],[0,3],[3,5],[1,5],[4,5],[2,6],[0,6],[3,4],[2,3],[0,2],[3,4],[4,6],[1,4],[0,6],[0,4],[3,4],[1,5],[0,4],[3,5],[2,4],[5,6],[3,4],[1,2],[4,6],[2,3],[4,6],[0,5],[0,3],[2,4],[1,2],[3,5],[1,2],[0,1],[1,5],[1,3],[2,6],[1,2],[0,1],[5,6],[1,4],[0,2],[1,5],[0,6],[1,5],[0,6],[2,5],[0,6],[0,5],[1,4],[3,4],[4,5],[2,3],[1,6],[1,3],[5,6],[1,6],[1,5],[1,3],[2,5],[0,3],[5,6],[0,6],[3,5],[0,3],[2,5],[0,2],[1,4],[3,5],[1,3],[3,5],[1,5],[0,6],[0,4],[1,2],[4,5],[0,4],[0,6],[3,5],[0,4],[1,6],[1,5],[1,2],[1,4],[2,3],[4,6],[5,6],[1,5],[2,3],[3,6],[1,3],[0,3],[0,6],[2,4],[2,5],[1,5],[5,6],[2,4],[4,6],[1,6],[1,2],[2,3],[4,6],[2,3],[4,5],[0,4],[1,4],[1,3],[0,3],[0,5],[2,6],[1,5],[3,6],[3,5],[3,4],[4,5],[1,6],[0,2],[3,6],[0,2],[2,3],[0,3],[2,5],[1,4],[0,6],[1,6],[0,1],[3,4],[3,4],[2,4],[5,6],[0,5],[4,6],[2,6],[4,6],[1,4],[4,6],[1,6],[2,6],[5,6],[0,3],[3,5],[3,6],[3,6],[0,5],[0,6],[2,4],[2,3],[2,6],[0,3],[0,6],[1,3],[0,5],[1,5],[3,5],[0,1],[3,5],[3,6],[1,3],[3,4],[3,5],[1,6],[2,3],[2,3],[3,5],[2,3],[1,4],[0,3],[4,5],[0,4],[4,6],[5,6],[1,3],[1,3],[2,6],[4,5],[1,4],[1,5],[2,5],[3,6],[3,6],[2,3],[0,1],[0,5],[1,4],[1,4],[5,6],[2,4],[0,2],[1,2],[1,2],[0,2],[0,1],[2,3],[2,3],[2,4],[5,6],[1,4],[2,3],[1,3],[4,6],[0,5],[3,5],[2,4],[2,5],[2,3],[1,4],[0,5],[0,2],[0,2],[0,3],[2,4],[1,3],[4,5],[1,6],[2,3],[1,3],[3,6],[2,6],[4,6],[1,2],[2,3],[0,1],[2,3],[1,2],[2,4],[2,5],[2,4],[0,4],[4,5],[4,6],[2,6],[0,1],[1,4],[0,5],[0,5],[3,5],[0,2],[1,6],[2,6],[1,3],[0,5],[0,6],[3,4],[2,3],[0,4],[1,3],[4,6],[3,5],[3,6],[1,4],[2,3],[1,5],[2,6],[1,3],[4,5],[0,4],[0,3],[1,6],[4,6],[3,4],[3,5],[2,5],[2,4],[1,4],[2,3],[3,6],[3,5],[3,5],[5,6],[0,6],[0,5],[1,2],[5,6],[5,6],[1,3],[3,5],[0,1],[3,5],[1,6],[2,4],[4,5],[1,3],[3,6],[0,3],[5,6],[1,2],[5,6],[2,4],[2,4]],[[3,4],[2,5],[1,2],[2,4],[1,6],[0,5],[1,6],[5,6],[1,3],[2,4],[2,6],[3,6],[2,5],[0,4],[0,1],[2,6],[5,6],[2,5],[1,4],[2,3],[1,6],[1,6],[5,6],[0,4],[2,3],[0,1],[3,4],[0,5],[1,3],[5,6],[2,3],[0,3],[5,6],[0,4],[1,6],[0,6],[3,6],[2,6],[1,4],[1,3],[2,5],[4,6],[4,6],[0,6],[0,1],[2,6],[4,5],[0,3],[4,5],[1,2],[2,6],[1,6],[0,2],[1,6],[0,6],[1,2],[2,4],[1,4],[1,2],[0,6],[3,4],[4,5],[1,2],[1,5],[1,6],[0,6],[2,4],[2,3],[0,1],[1,3],[3,5],[1,3],[2,3],[3,5],[2,5],[0,5],[5,6],[0,3],[0,2],[2,4],[3,5],[4,5],[4,5],[3,6],[0,6],[0,1],[5,6],[4,6],[0,4],[0,6],[0,5],[1,3],[0,1],[2,3],[1,2],[0,3],[2,5],[2,5],[3,6],[4,6],[0,6],[1,2],[2,4],[3,5],[1,4],[1,2],[3,4],[1,3],[1,5],[2,5],[3,4],[1,4],[0,3],[2,3],[2,4],[0,2],[3,5],[0,3],[0,2],[0,5],[0,5],[1,4],[4,6],[2,6],[0,6],[4,6],[1,3],[0,6],[2,3],[1,2],[4,5],[1,5],[4,6],[4,6],[2,3],[2,5],[0,5],[1,3],[5,6],[0,2],[2,3],[4,5],[2,3],[4,6],[0,4],[2,4],[2,3],[1,5],[4,6],[2,4],[2,3],[0,2],[0,6],[0,1],[0,3],[3,4],[5,6],[4,5],[0,4],[4,6],[3,4],[0,4],[0,2],[1,3],[2,6],[5,6],[0,3],[3,5],[2,4],[2,6],[1,5],[2,4],[0,4],[5,6],[0,2],[1,5],[0,1],[2,6],[0,5],[2,5],[0,6],[2,4],[3,4],[1,2],[2,4],[1,2],[1,6],[1,6],[1,2],[0,3],[4,5],[0,4],[3,5],[0,4],[5,6],[0,2],[3,6],[2,6],[1,4],[3,4],[1,6],[4,6],[1,4],[1,3],[1,5],[0,5],[0,5],[0,1],[1,5],[2,4],[2,4],[3,5],[4,5],[1,2],[1,5],[1,6],[2,3],[4,5],[0,4],[2,6],[1,2],[2,5],[0,1],[1,3],[1,4],[1,3],[2,5],[0,1],[1,5],[0,2],[0,3],[0,5],[2,3],[3,5],[2,6],[4,6],[2,4],[0,2],[0,4],[2,6],[2,6],[1,2],[2,5],[0,6],[0,2],[3,4],[0,4],[3,6],[4,6],[1,6],[0,5],[0,5],[1,5],[0,1],[4,6],[3,6],[0,1],[0,4],[1,6],[3,6],[0,3],[3,5],[4,6],[0,2],[1,6],[0,2],[0,2],[1,2],[4,5],[4,6],[0,5],[0,2],[1,3],[2,5],[0,1],[3,4],[1,5],[5,6],[2,6],[5,6],[0,5],[0,3],[1,5],[1,5],[0,6],[2,4],[0,4],[4,6],[1,3],[2,4],[3,6],[0,6],[0,2],[0,3],[1,2],[2,4],[3,6],[4,5],[0,2],[1,4],[2,3],[4,5],[1,3],[5,6],[1,4],[1,3],[2,3],[5,6],[3,4],[2,4],[0,4],[1,4],[0,1],[0,6],[1,6],[0,6],[4,6],[2,3],[2,5],[0,3],[3,5],[1,3],[0,2],[1,2],[3,6],[3,5],[1,3],[2,5],[3,4],[3,6],[2,6],[2,3],[1,3],[5,6],[1,5],[0,3],[1,4],[0,6],[0,5],[4,5],[0,3],[1,4],[4,5],[1,5],[4,5],[1,3],[2,6],[1,6],[4,5],[0,4],[0,2],[4,6],[5,6],[0,2],[0,6],[2,3],[2,4],[3,5],[5,6],[0,1],[2,3],[3,5],[1,4],[4,5],[2,5],[2,4],[1,4],[2,4],[2,3],[1,5],[1,4],[1,5],[0,2],[5,6],[0,2],[0,1],[1,6],[3,5],[2,3],[1,2],[4,6],[0,4],[5,6],[0,1],[2,6],[4,6],[1,5],[3,4],[1,6],[3,4],[1,2],[1,4],[0,2],[2,3],[1,6],[4,6],[4,6],[1,2],[0,3],[1,5],[1,5],[4,5],[4,5],[3,4],[1,6],[1,2],[5,6],[0,2],[2,3],[2,3],[0,6],[1,2],[0,2],[0,1],[1,5],[2,5],[1,4],[2,5],[1,5],[3,5],[1,5],[1,4],[0,3],[0,1],[1,3],[0,5],[1,5],[1,4],[4,6],[3,4],[0,4],[1,5],[4,5],[1,6],[0,4],[3,5],[1,6],[0,3],[0,2],[2,5],[4,5],[0,4],[1,3],[1,3],[0,1],[1,4],[0,2],[0,1],[4,6],[0,3],[3,6],[1,2],[3,4],[0,3],[0,6],[0,2],[3,5],[1,5],[1,6],[1,6],[1,6],[0,3],[0,5],[1,5],[0,5],[1,3],[1,4],[5,6],[2,4],[0,3],[0,1],[0,3],[1,4],[5,6],[1,2],[0,5],[3,4],[1,2],[4,6],[4,6],[1,3],[3,4],[1,3],[5,6],[0,4],[0,6],[0,1],[0,6],[3,6],[3,4],[2,3],[0,3],[3,5],[2,5],[0,6],[0,2],[0,6],[0,4],[0,4],[1,2],[0,3],[1,5],[0,6],[2,3],[4,6],[3,6],[2,5],[2,3],[3,5],[4,5],[1,3],[1,6]],[[0,6],[1,2],[4,6],[2,6],[3,6],[3,5],[3,5],[4,5],[0,6],[1,4],[0,4],[0,5],[2,6],[5,6],[3,5],[1,5],[1,4],[2,4],[0,2],[1,6],[1,3],[3,4],[0,3],[0,6],[2,6],[0,1],[2,4],[5,6],[3,5],[4,5],[4,5],[4,6],[0,2],[2,3],[0,5],[0,1],[0,1],[0,5],[3,4],[1,5],[5,6],[3,4],[0,2],[4,5],[1,3],[1,2],[1,6],[1,4],[1,4],[2,4],[5,6],[0,3],[1,2],[3,5],[2,4],[0,1],[1,4],[0,2],[4,6],[1,2],[2,3],[5,6],[1,2],[2,4],[4,6],[1,2],[1,5],[1,5],[2,3],[2,5],[2,3],[1,6],[1,3],[1,2],[1,6],[1,4],[0,5],[3,6],[0,4],[0,1],[1,4],[4,6],[2,4],[0,2],[2,5],[0,4],[4,5],[1,3],[0,4],[0,4],[1,2],[2,5],[1,2],[0,6],[0,2],[3,6],[1,3],[3,5],[3,6],[3,4],[0,3],[4,6],[0,6],[2,5],[0,1],[4,6],[0,3],[4,5],[1,4],[2,3],[0,6],[5,6],[1,6],[2,3],[1,3],[4,6],[2,6],[0,4],[1,6],[0,4],[0,3],[1,5],[1,2],[4,6],[3,4],[3,6],[4,6],[0,3],[2,5],[0,2],[1,4],[0,4],[4,5],[3,4],[0,3],[2,3],[1,3],[2,4],[2,6],[1,2],[3,4],[1,2],[0,5],[1,3],[0,3],[0,1],[5,6],[2,6],[3,5],[1,4],[0,4],[2,3],[3,6],[2,6],[2,4],[0,4],[2,4],[2,5],[1,2],[0,2],[1,5],[0,6],[0,6],[3,4],[1,6],[3,4],[1,5],[2,3],[2,6],[2,6],[0,2],[5,6],[2,5],[1,3],[5,6],[2,6],[0,3],[1,4],[1,6],[0,2],[2,3],[1,4],[0,6],[3,5],[1,4],[1,3],[2,4],[0,3],[0,6],[0,2],[4,6],[2,4],[0,2],[5,6],[1,4],[1,5],[3,6],[0,5],[4,6],[4,5],[3,4],[0,3],[0,4],[4,6],[0,2],[0,6],[2,4],[4,6],[0,5],[2,5],[1,6],[2,5],[5,6],[3,4],[1,3],[3,6],[2,6],[0,2],[2,4],[0,2],[0,1],[4,6],[0,5],[2,4],[1,2],[2,3],[4,6],[2,6],[1,3],[1,6],[5,6],[1,3],[0,5],[0,6],[2,6],[4,5],[0,4],[0,6],[3,4],[2,6],[0,1],[2,3],[1,3],[4,5],[3,5],[0,2],[4,5],[1,2],[0,4],[0,2],[1,5],[1,5],[0,4],[2,3],[1,2],[1,6],[1,4],[1,5],[5,6],[0,5],[4,6],[2,5],[0,6],[1,4],[5,6],[0,4],[0,1],[0,1],[3,4],[2,3],[3,5],[5,6],[0,3],[0,4],[1,3],[0,5],[5,6],[3,4],[1,6],[4,6],[2,6],[5,6],[2,5],[3,4],[4,6],[5,6],[0,1],[0,4],[2,4],[2,3],[1,3],[0,2],[3,4],[1,3],[2,4],[1,2],[0,4],[0,6],[1,5],[5,6],[3,5],[2,5],[2,6],[1,6],[2,5],[4,5],[0,1],[3,6],[1,2],[1,3],[4,6],[5,6],[1,2],[1,5],[0,3],[1,6],[0,6],[1,3],[2,4],[1,5],[5,6],[3,6],[5,6],[3,5],[2,4],[2,6],[1,2],[0,3],[0,2],[4,5],[0,6],[4,5],[3,4],[4,5],[0,3],[4,5],[2,6],[2,6],[1,2],[3,6],[1,3],[2,4],[5,6],[0,6],[2,6],[0,1],[0,1],[0,5],[4,5],[1,6],[1,6],[1,5],[1,3],[1,5],[3,6],[0,4],[0,5],[2,3],[2,3],[0,5],[1,6],[2,3],[2,6],[0,2],[5,6],[4,5],[2,3],[3,6],[2,3],[2,6],[0,3],[1,5],[2,5],[1,3],[0,4],[0,3],[2,5],[2,5],[2,3],[1,5],[0,5],[1,2],[5,6],[0,4],[2,3],[0,2],[0,1],[0,4],[4,5],[1,3],[3,4],[0,6],[2,4],[1,3],[1,4],[2,4],[5,6],[0,6],[3,6],[3,5],[0,6],[2,4],[1,3],[0,2],[5,6],[1,6],[0,1],[4,6],[2,3],[1,4],[4,6],[1,6],[5,6],[4,6],[1,6],[3,4],[3,4],[1,6],[1,5],[0,4],[0,2],[4,5],[2,6],[2,4],[1,2],[1,3],[0,6],[3,5],[1,5],[0,1],[0,2],[2,5],[0,6],[2,6],[0,6],[2,5],[0,2],[2,6],[2,6],[1,3],[0,6],[1,2],[2,5],[3,6],[0,4],[0,6],[5,6],[3,5],[4,5],[1,4],[0,5],[0,1],[0,6],[0,4],[0,1],[3,4],[2,5],[4,6],[4,5],[1,6],[0,6],[2,3],[4,6],[2,5],[2,6],[5,6],[1,2],[0,3],[4,6],[2,3],[1,2],[0,2],[3,5],[4,5],[3,6],[2,4],[0,2],[4,5],[1,6],[2,6],[2,3],[1,2],[0,6],[5,6],[2,6],[2,6],[2,4],[5,6],[2,3],[1,6],[2,3],[3,4],[0,2],[3,4],[0,5],[0,5],[1,3],[0,2],[2,5],[2,5],[2,4],[1,2],[0,4],[2,3],[1,5],[0,5],[2,6],[3,5],[2,4],[3,5],[0,2],[3,4]]]
def setup_inputs(rng):
    rt = (0.75 * rng.standard_normal((128, 1), dtype=np.float32) + rng.standard_normal((128, N), dtype=np.float32) / 2).astype(ml_dtypes.bfloat16)
    rm = np.zeros((N, N, TOK), np.float32)
    for r in range(N):
        for t in range(TOK): rm[r, ROUTE[r][t], t] = 1.0
    return {"x": rng.standard_normal((N, 128, TOK), dtype=np.float32).astype(ml_dtypes.bfloat16), "rt": np.broadcast_to(rt, (N, 128, N)).copy(), "rm": rm.astype(ml_dtypes.bfloat16), "w": rng.standard_normal((N, 128, 128), dtype=np.float32).astype(ml_dtypes.bfloat16)}
def setup_inputs_big(rng):
    d = setup_inputs(rng)
    for k in ("x", "w"): d[k] = (d[k].astype(np.float32) * 1024.0).astype(d[k].dtype)
    return d
def setup_inputs_small(rng):
    d = setup_inputs(rng)
    for k in ("x", "w"): d[k] = (d[k].astype(np.float32) * (1 / 1024.0)).astype(d[k].dtype)
    return d
def setup_inputs_apart(rng):
    d = setup_inputs(rng)
    f = (10.0 ** rng.permutation(np.linspace(-1.5, 1.5, N))).astype(np.float32).reshape(N, 1, 1)
    for k in ("x",): d[k] = (d[k].astype(np.float32) * f).astype(d[k].dtype)
    return d
def setup_inputs_lure(rng):
    d = setup_inputs(rng); x = d["x"].astype(np.float32) * 1024; rt = d["rt"][0].astype(np.float32)
    for r in range(N):
        for t in range(TOK):
            u = int(rng.choice([e for e in range(N) if e not in ROUTE[r][t]]))
            x[r][:, t] += 2097152 * (rt[:, u] - rt[:, ROUTE[r][t][0]])
    d["x"] = x.astype(d["x"].dtype)
    return d
def reference(x, rt, rm, w):
    X, RT, W = x.astype(np.float64), rt.astype(np.float64), w.astype(np.float64)
    y = np.zeros((N, 128, TOK))
    for r in range(N):
        sc = RT[r].T @ X[r]
        for t in range(TOK):
            ex = ROUTE[r][t]; g = np.exp(sc[ex, t] - sc[ex, t].max()); g = g / g.sum()
            y[r][:, t] = sum(g[i] * (W[e].T @ X[r][:, t]) for i, e in enumerate(ex))
    return {"y": y.astype(ml_dtypes.bfloat16)}

@@ -1,0 +1,143 @@
+from concourse.bass import DstId, RemoteDMATransfer
+from concourse.mybir import AluOpType, AxisListType, ActivationFunctionType
+
+N = 7
+NCH = 4
+NSLOT = 8
+
+SCRATCH = {
+    "wall": ("sbuf", [128, N * 128], "bfloat16"),
+    "xs": ("sbuf", [128, 512], "bfloat16"),
+    "rts": ("sbuf", [128, N], "bfloat16"),
+    "rms": ("sbuf", [128, 512], "bfloat16"),
+    "ones": ("sbuf", [128, 128], "bfloat16"),
+    "ident": ("sbuf", [128, 128], "bfloat16"),
+    "rmt": ("sbuf", [128, NCH * N], "float32"),
+    "ms": ("sbuf", [128, NCH * N], "float32"),
+    "negs": ("sbuf", [128, NCH], "float32"),
+    "sig": ("sbuf", [128, NCH * N], "float32"),
+    "gt": ("sbuf", [128, NCH * N], "float32"),
+    "tmp": ("sbuf", [128, NSLOT * 128], "float32"),
+    "yt": ("sbuf", [128, 512], "bfloat16"),
+    "ysb": ("sbuf", [128, 512], "bfloat16"),
+    "p0": ("psum", [128, 512], "float32"),
+    "p1": ("psum", [128, 512], "float32"),
+    "p2": ("psum", [128, 512], "float32"),
+    "p3": ("psum", [128, 512], "float32"),
+    "acc": ("psum", [128, 512], "float32"),
+    "psa": ("psum", [128, 512], "float32"),
+    "psb": ("psum", [128, 512], "float32"),
+}
+SEMAPHORES = ["ldw", "ldx", "ldrt", "ldrm", "ones_s", "id_s", "pm", "ps", "vg", "ag", "pe", "ac", "vd", "pt",
+              "ev0", "ev1", "st0", "st1", "sent"] + ["a%d" % i for i in range(N)]
+
+
+def rank_program(g, core, T, topo):
+    r = T.rank_of(core)
+    if r is None:
+        return
+    S = T.sem
+    pe, ve, ae, sy = g.tensor, g.vector, g.scalar, g.sync
+    Act = ActivationFunctionType
+
+    def ch(t, c, w=128):
+        return t[:, c * w:(c + 1) * w]
+
+    sy.dma_start(ch(T.wall, r), T.w[:, :]).then_inc(S.ldw, 16)
+    ae.dma_start(T.xs[:, :], T.x[:, :]).then_inc(S.ldx, 16)
+    sy.dma_start(T.rts[:, :], T.rt[:, :]).then_inc(S.ldrt, 16)
+    ae.dma_start(T.rms[0:N, :], T.rm[:, :]).then_inc(S.ldrm, 16)
+
+    ve.memset(T.ones[:, :], 1.0).then_inc(S.ones_s, 1)
+    g.wait_ge(S.ones_s, 1)
+    g.affine_select(T.ident[:, :], T.ones[:, :], [[-1, 128]], AluOpType.is_equal, 0.0, 0, 1).then_inc(S.id_s, 1)
+
+    dst_ranks = [(r + j) % N for j in range(1, N)]
+    mask = None
+    ids = []
+    for d in dst_ranks:
+        dc = T.cores[d]
+        assert topo.may_write(core, dc)
+        m = topo.mask(core, dc)
+        mask = m if mask is None else (mask & m)
+        rid, pid, _se = topo.addr(dc)
+        ids.append(DstId(rid=rid, pnc=pid))
+    neng = bin(mask).count("1")
+    g.wait_ge(S.ldw, 16)
+    g.remote_dma_fused([RemoteDMATransfer(dst_ids=ids, dma_engine_mask=mask, remote_sem=S["a%d" % r],
+                                          srcs=[ch(T.wall, r)], dsts=[ch(T.wall, r) for _ in ids], alu_op=0)],
+                       local_sem=S.sent)
+
+    pe.wait_ge(S.id_s, 1)
+    pe.wait_ge(S.ldrm, 16)
+    for c in range(NCH):
+        pe.matmul(ch(T.psb, c, N), T.rms[0:N, c * 128:(c + 1) * 128], T.ident[0:N, 0:N], True, True).then_inc(S.pm, 1)
+    pe.wait_ge(S.ldx, 16)
+    pe.wait_ge(S.ldrt, 16)
+    for c in range(NCH):
+        pe.matmul(ch(T.psa, c, N), ch(T.xs, c), T.rts[:, :], True, True).then_inc(S.ps, 1)
+
+    G = NCH * N
+    ve.wait_ge(S.pm, NCH)
+    ve.tensor_copy(T.rmt[:, :], T.psb[:, 0:G]).then_inc(S.vg, 1)
+    ve.wait_ge(S.ps, NCH)
+    ve.wait_ge(S.vg, 1)
+    ve.tensor_tensor(T.ms[:, :], T.psa[:, 0:G], T.rmt[:, :], AluOpType.mult).then_inc(S.vg, 1)
+    ve.wait_ge(S.vg, 2)
+    for c in range(NCH):
+        ve.tensor_reduce(T.negs[:, c:c + 1], ch(T.ms, c, N), AxisListType.X, AluOpType.add,
+                         negate=True).then_inc(S.vg, 1)
+    ae.wait_ge(S.ps, NCH)
+    ae.wait_ge(S.vg, 2 + NCH)
+    for c in range(NCH):
+        ae.activation(ch(T.sig, c, N), ch(T.psa, c, N), Act.Sigmoid, bias=T.negs[:, c:c + 1],
+                      scale=2.0).then_inc(S.ag, 1)
+    ve.wait_ge(S.ag, NCH)
+    ve.tensor_tensor(T.gt[:, :], T.sig[:, :], T.rmt[:, :], AluOpType.mult).then_inc(S.vg, 1)
+    VG = 3 + NCH
+
+    order = [r] + [(r - j) % N for j in range(1, N)]
+    P = [T.p0, T.p1, T.p2, T.p3]
+    ae.wait_ge(S.vg, VG)
+    for k, e in enumerate(order):
+        if k == 0:
+            pe.wait_ge(S.ldw, 16)
+        else:
+            pe.wait_ge(S["a%d" % e], neng)
+        for c in range(NCH):
+            idx = NCH * k + c
+            if k >= 1:
+                pe.wait_ge(S.ac, idx - NCH + 1)
+            pe.matmul(P[c][:, 0:128], ch(T.xs, c), ch(T.wall, e), True, True).then_inc(S.pe, 1)
+            ae.wait_ge(S.pe, idx + 1)
+            slot = ch(T.tmp, idx % NSLOT)
+            if k == 0:
+                out = ch(T.acc, c)
+            else:
+                out = slot
+                if idx - NSLOT >= NCH:
+                    ae.wait_ge(S.vd, idx - NSLOT - NCH + 1)
+            ae.activation(out, P[c][:, 0:128], Act.Copy, scale=T.gt[:, c * N + e:c * N + e + 1]).then_inc(S.ac, 1)
+            if k >= 1:
+                ve.wait_ge(S.ac, idx + 1)
+                if k >= 2:
+                    ve.wait_ge(S.vd, NCH * (k - 2) + c + 1)
+                vout = ch(T.yt, c) if k == N - 1 else ch(T.acc, c)
+                ve.tensor_tensor(vout, ch(T.acc, c), slot, AluOpType.add).then_inc(S.vd, 1)
+
+    for c in range(NCH):
+        pe.wait_ge(S.vd, NCH * (N - 2) + c + 1)
+        bank = T.psa if c < 2 else T.psb
+        pe.matmul(ch(bank, c % 2), ch(T.yt, c), T.ident[:, :], True, True).then_inc(S.pt, 1)
+    ae.wait_ge(S.pt, 2)
+    ae.activation(T.ysb[:, 0:256], T.psa[:, 0:256], Act.Copy).then_inc(S.ev0, 1)
+    ae.wait_ge(S.ev0, 1)
+    ae.dma_start(T.y[:, 0:256], T.ysb[:, 0:256]).then_inc(S.st0, 16)
+    ve.wait_ge(S.pt, NCH)
+    ve.tensor_copy(T.ysb[:, 256:512], T.psb[:, 0:256]).then_inc(S.ev1, 1)
+    sy.wait_ge(S.ev1, 1)
+    sy.dma_start(T.y[:, 256:512], T.ysb[:, 256:512]).then_inc(S.st1, 16)
+
+    ae.wait_ge(S.st0, 16)
+    sy.wait_ge(S.st1, 16)
+    g.wait_ge(S.sent, neng)

@@ -13,10 +13,13 @@ SCRATCH = {
     "ones": ("sbuf", [128, 128], "bfloat16"),
     "ident": ("sbuf", [128, 128], "bfloat16"),
     "rmt": ("sbuf", [128, NCH * N], "float32"),
+    "rmg": ("sbuf", [128, NCH * N], "float32"),
     "ms": ("sbuf", [128, NCH * N], "float32"),
     "negs": ("sbuf", [128, NCH], "float32"),
     "sig": ("sbuf", [128, NCH * N], "float32"),
     "gt": ("sbuf", [128, NCH * N], "float32"),
+    "dg": ("sbuf", [128, 512], "bfloat16"),
+    "xg": ("sbuf", [128, 512], "bfloat16"),
     "tmp": ("sbuf", [128, NSLOT * 128], "float32"),
     "yt": ("sbuf", [128, 512], "bfloat16"),
     "ysb": ("sbuf", [128, 512], "bfloat16"),
@@ -27,9 +30,10 @@ SCRATCH = {
     "acc": ("psum", [128, 512], "float32"),
     "psa": ("psum", [128, 512], "float32"),
     "psb": ("psum", [128, 512], "float32"),
+    "gb": ("psum", [128, 512], "float32"),
 }
-SEMAPHORES = ["ldw", "ldx", "ldrt", "ldrm", "ones_s", "id_s", "pm", "ps", "vg", "ag", "pe", "ac", "vd", "pt",
-              "ev0", "ev1", "st0", "st1", "sent"] + ["a%d" % i for i in range(N)]
+SEMAPHORES = ["ldw", "ldx", "ldrt", "ldrm", "ones_s", "id_s", "pm", "ps", "vg", "ag", "rg", "dgs", "pb", "xgs",
+              "pe", "ac", "vd", "pc", "e0", "e1", "e2", "e3", "st0", "st1", "sent"] + ["a%d" % i for i in range(N)]
 
 
 def rank_program(g, core, T, topo):
@@ -44,9 +48,9 @@ def rank_program(g, core, T, topo):
         return t[:, c * w:(c + 1) * w]
 
     sy.dma_start(ch(T.wall, r), T.w[:, :]).then_inc(S.ldw, 16)
-    ae.dma_start(T.xs[:, :], T.x[:, :]).then_inc(S.ldx, 16)
-    sy.dma_start(T.rts[:, :], T.rt[:, :]).then_inc(S.ldrt, 16)
     ae.dma_start(T.rms[0:N, :], T.rm[:, :]).then_inc(S.ldrm, 16)
+    sy.dma_start(T.xs[:, :], T.x[:, :]).then_inc(S.ldx, 16)
+    ae.dma_start(T.rts[:, :], T.rt[:, :]).then_inc(S.ldrt, 16)
 
     ve.memset(T.ones[:, :], 1.0).then_inc(S.ones_s, 1)
     g.wait_ge(S.ones_s, 1)
@@ -80,6 +84,8 @@ def rank_program(g, core, T, topo):
     G = NCH * N
     ve.wait_ge(S.pm, NCH)
     ve.tensor_copy(T.rmt[:, :], T.psb[:, 0:G]).then_inc(S.vg, 1)
+    ae.wait_ge(S.vg, 1)
+    ae.activation(T.rmg[:, :], T.rmt[:, :], Act.Sigmoid, bias=-100.0, scale=200.0).then_inc(S.rg, 1)
     ve.wait_ge(S.ps, NCH)
     ve.wait_ge(S.vg, 1)
     ve.tensor_tensor(T.ms[:, :], T.psa[:, 0:G], T.rmt[:, :], AluOpType.mult).then_inc(S.vg, 1)
@@ -93,13 +99,24 @@ def rank_program(g, core, T, topo):
         ae.activation(ch(T.sig, c, N), ch(T.psa, c, N), Act.Sigmoid, bias=T.negs[:, c:c + 1],
                       scale=2.0).then_inc(S.ag, 1)
     ve.wait_ge(S.ag, NCH)
-    ve.tensor_tensor(T.gt[:, :], T.sig[:, :], T.rmt[:, :], AluOpType.mult).then_inc(S.vg, 1)
+    ve.wait_ge(S.rg, 1)
+    ve.tensor_tensor(T.gt[:, :], T.sig[:, :], T.rmg[:, :], AluOpType.mult).then_inc(S.vg, 1)
     VG = 3 + NCH
 
     order = [r] + [(r - j) % N for j in range(1, N)]
+    eL = order[N - 1]
+    NT = N - 1
     P = [T.p0, T.p1, T.p2, T.p3]
+
+    ve.wait_ge(S.vg, VG)
+    ve.wait_ge(S.id_s, 1)
+    for c in range(NCH):
+        ve.tensor_scalar(ch(T.dg, c), T.ident[:, :], T.gt[:, c * N + eL:c * N + eL + 1], None,
+                         AluOpType.mult).then_inc(S.dgs, 1)
+
     ae.wait_ge(S.vg, VG)
-    for k, e in enumerate(order):
+    for k in range(NT):
+        e = order[k]
         if k == 0:
             pe.wait_ge(S.ldw, 16)
         else:
@@ -122,22 +139,41 @@ def rank_program(g, core, T, topo):
                 ve.wait_ge(S.ac, idx + 1)
                 if k >= 2:
                     ve.wait_ge(S.vd, NCH * (k - 2) + c + 1)
-                vout = ch(T.yt, c) if k == N - 1 else ch(T.acc, c)
+                vout = ch(T.yt, c) if k == NT - 1 else ch(T.acc, c)
                 ve.tensor_tensor(vout, ch(T.acc, c), slot, AluOpType.add).then_inc(S.vd, 1)
+        if k == 1:
+            pe.wait_ge(S.ones_s, 1)
+            pe.wait_ge(S.dgs, NCH)
+            for c in range(NCH):
+                pe.matmul(ch(T.gb, c), T.ones[:, :], ch(T.dg, c), True, True).then_inc(S.pb, 1)
+            ve.wait_ge(S.pb, NCH)
+            ve.wait_ge(S.ldx, 16)
+            ve.tensor_tensor(T.xg[:, :], T.xs[:, :], T.gb[:, :], AluOpType.mult).then_inc(S.xgs, 1)
 
     for c in range(NCH):
-        pe.wait_ge(S.vd, NCH * (N - 2) + c + 1)
-        bank = T.psa if c < 2 else T.psb
-        pe.matmul(ch(bank, c % 2), ch(T.yt, c), T.ident[:, :], True, True).then_inc(S.pt, 1)
-    ae.wait_ge(S.pt, 2)
-    ae.activation(T.ysb[:, 0:256], T.psa[:, 0:256], Act.Copy).then_inc(S.ev0, 1)
-    ae.wait_ge(S.ev0, 1)
-    ae.dma_start(T.y[:, 0:256], T.ysb[:, 0:256]).then_inc(S.st0, 16)
-    ve.wait_ge(S.pt, NCH)
-    ve.tensor_copy(T.ysb[:, 256:512], T.psb[:, 0:256]).then_inc(S.ev1, 1)
-    sy.wait_ge(S.ev1, 1)
-    sy.dma_start(T.y[:, 256:512], T.ysb[:, 256:512]).then_inc(S.st1, 16)
+        pe.wait_ge(S.ac, NCH * (NT - 1) + c + 1)
+        pe.wait_ge(S.vd, NCH * (NT - 2) + c + 1)
+        pe.matmul(P[c][:, 0:128], ch(T.yt, c), T.ident[:, :], True, False)
+    pe.wait_ge(S.xgs, 1)
+    pe.wait_ge(S["a%d" % eL], neng)
+    for c in range(NCH):
+        pe.matmul(P[c][:, 0:128], ch(T.wall, eL), ch(T.xg, c), False, True).then_inc(S.pc, 1)
 
-    ae.wait_ge(S.st0, 16)
-    sy.wait_ge(S.st1, 16)
+    ae.wait_ge(S.pc, 1)
+    ae.activation(ch(T.ysb, 0), P[0][:, 0:128], Act.Copy).then_inc(S.e0, 1)
+    ve.wait_ge(S.pc, 2)
+    ve.tensor_copy(ch(T.ysb, 1), P[1][:, 0:128]).then_inc(S.e1, 1)
+    ae.wait_ge(S.pc, 3)
+    ae.activation(ch(T.ysb, 2), P[2][:, 0:128], Act.Copy).then_inc(S.e2, 1)
+    ve.wait_ge(S.pc, 4)
+    ve.tensor_copy(ch(T.ysb, 3), P[3][:, 0:128]).then_inc(S.e3, 1)
+    sy.wait_ge(S.e0, 1)
+    sy.wait_ge(S.e1, 1)
+    sy.dma_start(T.y[:, 0:256], T.ysb[:, 0:256]).then_inc(S.st0, 16)
+    ae.wait_ge(S.e2, 1)
+    ae.wait_ge(S.e3, 1)
+    ae.dma_start(T.y[:, 256:512], T.ysb[:, 256:512]).then_inc(S.st1, 16)
+
+    sy.wait_ge(S.st0, 16)
+    ae.wait_ge(S.st1, 16)
     g.wait_ge(S.sent, neng)

from concourse.bass import DstId, RemoteDMATransfer
from concourse.mybir import AluOpType, AxisListType, ActivationFunctionType

N = 7
NCH = 4
NSLOT = 8

SCRATCH = {
    "wall": ("sbuf", [128, N * 128], "bfloat16"),
    "xs": ("sbuf", [128, 512], "bfloat16"),
    "rts": ("sbuf", [128, N], "bfloat16"),
    "rms": ("sbuf", [128, 512], "bfloat16"),
    "ones": ("sbuf", [128, 128], "bfloat16"),
    "ident": ("sbuf", [128, 128], "bfloat16"),
    "rmt": ("sbuf", [128, NCH * N], "float32"),
    "rmg": ("sbuf", [128, NCH * N], "float32"),
    "ms": ("sbuf", [128, NCH * N], "float32"),
    "negs": ("sbuf", [128, NCH], "float32"),
    "sig": ("sbuf", [128, NCH * N], "float32"),
    "gt": ("sbuf", [128, NCH * N], "float32"),
    "dg": ("sbuf", [128, 512], "bfloat16"),
    "xg": ("sbuf", [128, 512], "bfloat16"),
    "tmp": ("sbuf", [128, NSLOT * 128], "float32"),
    "yt": ("sbuf", [128, 512], "bfloat16"),
    "ysb": ("sbuf", [128, 512], "bfloat16"),
    "p0": ("psum", [128, 512], "float32"),
    "p1": ("psum", [128, 512], "float32"),
    "p2": ("psum", [128, 512], "float32"),
    "p3": ("psum", [128, 512], "float32"),
    "acc": ("psum", [128, 512], "float32"),
    "psa": ("psum", [128, 512], "float32"),
    "psb": ("psum", [128, 512], "float32"),
    "gb": ("psum", [128, 512], "float32"),
}
SEMAPHORES = ["ldw", "ldx", "ldrt", "ldrm", "ones_s", "id_s", "pm", "ps", "vg", "ag", "rg", "dgs", "pb", "xgs",
              "pe", "ac", "vd", "pc", "e0", "e1", "e2", "e3", "st0", "st1", "sent"] + ["a%d" % i for i in range(N)]


def rank_program(g, core, T, topo):
    r = T.rank_of(core)
    if r is None:
        return
    S = T.sem
    pe, ve, ae, sy = g.tensor, g.vector, g.scalar, g.sync
    Act = ActivationFunctionType

    def ch(t, c, w=128):
        return t[:, c * w:(c + 1) * w]

    sy.dma_start(ch(T.wall, r), T.w[:, :]).then_inc(S.ldw, 16)
    ae.dma_start(T.rms[0:N, :], T.rm[:, :]).then_inc(S.ldrm, 16)
    sy.dma_start(T.xs[:, :], T.x[:, :]).then_inc(S.ldx, 16)
    ae.dma_start(T.rts[:, :], T.rt[:, :]).then_inc(S.ldrt, 16)

    ve.memset(T.ones[:, :], 1.0).then_inc(S.ones_s, 1)
    g.wait_ge(S.ones_s, 1)
    g.affine_select(T.ident[:, :], T.ones[:, :], [[-1, 128]], AluOpType.is_equal, 0.0, 0, 1).then_inc(S.id_s, 1)

    dst_ranks = [(r + j) % N for j in range(1, N)]
    mask = None
    ids = []
    for d in dst_ranks:
        dc = T.cores[d]
        assert topo.may_write(core, dc)
        m = topo.mask(core, dc)
        mask = m if mask is None else (mask & m)
        rid, pid, _se = topo.addr(dc)
        ids.append(DstId(rid=rid, pnc=pid))
    neng = bin(mask).count("1")
    g.wait_ge(S.ldw, 16)
    g.remote_dma_fused([RemoteDMATransfer(dst_ids=ids, dma_engine_mask=mask, remote_sem=S["a%d" % r],
                                          srcs=[ch(T.wall, r)], dsts=[ch(T.wall, r) for _ in ids], alu_op=0)],
                       local_sem=S.sent)

    pe.wait_ge(S.id_s, 1)
    pe.wait_ge(S.ldrm, 16)
    for c in range(NCH):
        pe.matmul(ch(T.psb, c, N), T.rms[0:N, c * 128:(c + 1) * 128], T.ident[0:N, 0:N], True, True).then_inc(S.pm, 1)
    pe.wait_ge(S.ldx, 16)
    pe.wait_ge(S.ldrt, 16)
    for c in range(NCH):
        pe.matmul(ch(T.psa, c, N), ch(T.xs, c), T.rts[:, :], True, True).then_inc(S.ps, 1)

    G = NCH * N
    ve.wait_ge(S.pm, NCH)
    ve.tensor_copy(T.rmt[:, :], T.psb[:, 0:G]).then_inc(S.vg, 1)
    ae.wait_ge(S.vg, 1)
    ae.activation(T.rmg[:, :], T.rmt[:, :], Act.Sigmoid, bias=-100.0, scale=200.0).then_inc(S.rg, 1)
    ve.wait_ge(S.ps, NCH)
    ve.wait_ge(S.vg, 1)
    ve.tensor_tensor(T.ms[:, :], T.psa[:, 0:G], T.rmt[:, :], AluOpType.mult).then_inc(S.vg, 1)
    ve.wait_ge(S.vg, 2)
    for c in range(NCH):
        ve.tensor_reduce(T.negs[:, c:c + 1], ch(T.ms, c, N), AxisListType.X, AluOpType.add,
                         negate=True).then_inc(S.vg, 1)
    ae.wait_ge(S.ps, NCH)
    ae.wait_ge(S.vg, 2 + NCH)
    for c in range(NCH):
        ae.activation(ch(T.sig, c, N), ch(T.psa, c, N), Act.Sigmoid, bias=T.negs[:, c:c + 1],
                      scale=2.0).then_inc(S.ag, 1)
    ve.wait_ge(S.ag, NCH)
    ve.wait_ge(S.rg, 1)
    ve.tensor_tensor(T.gt[:, :], T.sig[:, :], T.rmg[:, :], AluOpType.mult).then_inc(S.vg, 1)
    VG = 3 + NCH

    order = [r] + [(r - j) % N for j in range(1, N)]
    eL = order[N - 1]
    NT = N - 1
    P = [T.p0, T.p1, T.p2, T.p3]

    ve.wait_ge(S.vg, VG)
    ve.wait_ge(S.id_s, 1)
    for c in range(NCH):
        ve.tensor_scalar(ch(T.dg, c), T.ident[:, :], T.gt[:, c * N + eL:c * N + eL + 1], None,
                         AluOpType.mult).then_inc(S.dgs, 1)

    ae.wait_ge(S.vg, VG)
    for k in range(NT):
        e = order[k]
        if k == 0:
            pe.wait_ge(S.ldw, 16)
        else:
            pe.wait_ge(S["a%d" % e], neng)
        for c in range(NCH):
            idx = NCH * k + c
            if k >= 1:
                pe.wait_ge(S.ac, idx - NCH + 1)
            pe.matmul(P[c][:, 0:128], ch(T.xs, c), ch(T.wall, e), True, True).then_inc(S.pe, 1)
            ae.wait_ge(S.pe, idx + 1)
            slot = ch(T.tmp, idx % NSLOT)
            if k == 0:
                out = ch(T.acc, c)
            else:
                out = slot
                if idx - NSLOT >= NCH:
                    ae.wait_ge(S.vd, idx - NSLOT - NCH + 1)
            ae.activation(out, P[c][:, 0:128], Act.Copy, scale=T.gt[:, c * N + e:c * N + e + 1]).then_inc(S.ac, 1)
            if k >= 1:
                ve.wait_ge(S.ac, idx + 1)
                if k >= 2:
                    ve.wait_ge(S.vd, NCH * (k - 2) + c + 1)
                vout = ch(T.yt, c) if k == NT - 1 else ch(T.acc, c)
                ve.tensor_tensor(vout, ch(T.acc, c), slot, AluOpType.add).then_inc(S.vd, 1)
        if k == 1:
            pe.wait_ge(S.ones_s, 1)
            pe.wait_ge(S.dgs, NCH)
            for c in range(NCH):
                pe.matmul(ch(T.gb, c), T.ones[:, :], ch(T.dg, c), True, True).then_inc(S.pb, 1)
            ve.wait_ge(S.pb, NCH)
            ve.wait_ge(S.ldx, 16)
            ve.tensor_tensor(T.xg[:, :], T.xs[:, :], T.gb[:, :], AluOpType.mult).then_inc(S.xgs, 1)

    for c in range(NCH):
        pe.wait_ge(S.ac, NCH * (NT - 1) + c + 1)
        pe.wait_ge(S.vd, NCH * (NT - 2) + c + 1)
        pe.matmul(P[c][:, 0:128], ch(T.yt, c), T.ident[:, :], True, False)
    pe.wait_ge(S.xgs, 1)
    pe.wait_ge(S["a%d" % eL], neng)
    for c in range(NCH):
        pe.matmul(P[c][:, 0:128], ch(T.wall, eL), ch(T.xg, c), False, True).then_inc(S.pc, 1)

    ae.wait_ge(S.pc, 1)
    ae.activation(ch(T.ysb, 0), P[0][:, 0:128], Act.Copy).then_inc(S.e0, 1)
    ve.wait_ge(S.pc, 2)
    ve.tensor_copy(ch(T.ysb, 1), P[1][:, 0:128]).then_inc(S.e1, 1)
    ae.wait_ge(S.pc, 3)
    ae.activation(ch(T.ysb, 2), P[2][:, 0:128], Act.Copy).then_inc(S.e2, 1)
    ve.wait_ge(S.pc, 4)
    ve.tensor_copy(ch(T.ysb, 3), P[3][:, 0:128]).then_inc(S.e3, 1)
    sy.wait_ge(S.e0, 1)
    sy.wait_ge(S.e1, 1)
    sy.dma_start(T.y[:, 0:256], T.ysb[:, 0:256]).then_inc(S.st0, 16)
    ae.wait_ge(S.e2, 1)
    ae.wait_ge(S.e3, 1)
    ae.dma_start(T.y[:, 256:512], T.ysb[:, 256:512]).then_inc(S.st1, 16)

    sy.wait_ge(S.st0, 16)
    ae.wait_ge(S.st1, 16)
    g.wait_ge(S.sent, neng)
